import numpy as np
import ml_dtypes


def mxq(x, axis, fmt="e4m3"):
    dtype, down = {"e4m3": (ml_dtypes.float8_e4m3fn, 7), "e5m2": (ml_dtypes.float8_e5m2, 14)}[fmt]
    v = np.moveaxis(np.asarray(x, np.float32).astype(ml_dtypes.bfloat16).astype(np.float64), axis, -1)
    blocks = v.reshape(v.shape[:-1] + (-1, 32))
    amax = np.abs(blocks).max(-1, keepdims=True)
    byte = np.maximum(np.where(amax > 0, np.frexp(amax)[1] - 1 + 127, 0) - down, 1)
    scale = np.exp2(byte - 127.0)
    codes = (blocks / scale).astype(np.float32).astype(dtype).astype(np.float64)
    return np.moveaxis((codes * scale).reshape(v.shape), -1, axis)


WIDE = False


def mx_kscale(k):
    if not WIDE:
        return np.ones(k)
    levels = np.array([10, -10, 5, -5, 0])
    if k % 512:
        return np.exp2(np.random.permutation(np.resize(levels, k // 32))).repeat(32)
    a = np.empty((k // 512, 16))
    for p in range(k // 512):
        a[p, :8] = np.random.permutation(np.resize(levels, 8))
        for g in range(8):
            far = levels[np.abs(levels - a[p, g]) >= 10]
            a[p, g + 8] = far[np.random.randint(len(far))]
    return np.exp2(a.ravel()).repeat(32)


def f64(x):
    return np.asarray(x).astype(np.float64)


def striped(idx):
    return np.tile(idx.reshape(-1, 16).T, (8, 1)).astype(np.uint16)


def unstriped(offs):
    return offs[:16].T.reshape(-1).astype(np.int64)


def striped8(idx):
    return np.concatenate([x.reshape(-1, 16).T for x in idx]).astype(np.uint16)


def runs(offs, k):
    lists = np.stack([offs[16 * r : 16 * r + 16].T.reshape(-1) for r in range(8)]).astype(np.int64)
    return lists[np.arange(k) % 512 // 64]


def pack_weight(w):
    k, n = w.shape
    w = f64(np.asarray(w, np.float32).astype(ml_dtypes.bfloat16)).reshape(k // 32, 32, n)
    amax = np.abs(w).max(1)
    byte = np.clip(np.where(amax > 0, np.frexp(amax)[1] - 1 + 127 - 7, 1), 1, 254)
    scaled = (w * np.exp2(127.0 - byte)[:, None, :]).reshape(k, n).astype(np.float32)
    words = np.ascontiguousarray(scaled.reshape(k // 512, 128, 4, n).transpose(0, 1, 3, 2)).astype(ml_dtypes.float8_e4m3fn).view(np.uint8)
    return words, np.ascontiguousarray(byte.astype(np.uint8).reshape(k // 512, 16, n))


def unpack_weight(words, scales):
    g, p, n, _ = words.shape
    vals = np.ascontiguousarray(words).view(ml_dtypes.float8_e4m3fn).astype(np.float64) * np.repeat(np.exp2(scales.astype(np.float64) - 127.0), 8, axis=1)[..., None]
    return vals.transpose(0, 1, 3, 2).reshape(g * 512, n)


E2M1 = np.array([0.0, 0.5, 1.0, 1.5, 2.0, 3.0, 4.0, 6.0, -0.0, -0.5, -1.0, -1.5, -2.0, -3.0, -4.0, -6.0])


def pack_fp4(w):
    k, n = w.shape
    w = f64(np.asarray(w, np.float32).astype(ml_dtypes.bfloat16)).reshape(k // 32, 32, n)
    amax = np.abs(w).max(1)
    mant, ex = np.frexp(amax / 6.0)
    byte = np.clip(np.where(amax > 0, np.where(mant > 0.5, ex, ex - 1) + 127, 1), 1, 254)
    scaled = (w * np.exp2(127.0 - byte)[:, None, :]).reshape(k, n).astype(np.float32)
    c = np.ascontiguousarray(scaled.reshape(k // 512, 128, 4, n).transpose(0, 1, 3, 2)).astype(ml_dtypes.float4_e2m1fn).view(np.uint8) & 0xF
    words = (c[..., 0::2] | (c[..., 1::2] << 4)).reshape(k // 512, 128, 2 * n)
    return np.ascontiguousarray(words), np.ascontiguousarray(byte.astype(np.uint8).reshape(k // 512, 16, n))


def unpack_fp4(words, scales):
    g, _, n = scales.shape
    words = np.ascontiguousarray(words).reshape(g, 128, n, 2)
    nib = np.empty((g, 128, n, 4), np.uint8)
    nib[..., 0::2] = words & 0xF
    nib[..., 1::2] = words >> 4
    vals = E2M1[nib] * np.repeat(np.exp2(scales.astype(np.float64) - 127.0), 8, axis=1)[..., None]
    return vals.transpose(0, 1, 3, 2).reshape(g * 512, n)


def relu(v):
    return np.maximum(v, 0.0)

def planes(y):
    n, m = y.shape
    v = y.astype(np.float32).astype(ml_dtypes.bfloat16).astype(np.float64).reshape(n // 32, 32, m)
    top = np.abs(v).max(1)
    byte = np.clip(np.where(top > 0, np.frexp(top)[1] - 1 + 127 - 7, 1), 1, 254)
    codes = (v * np.exp2(127.0 - byte)[:, None, :]).reshape(n, m).astype(np.float32).astype(ml_dtypes.float8_e4m3fn).view(np.uint8)
    words = codes.reshape(n // 512, 128, 4, m).transpose(0, 1, 3, 2)
    return np.ascontiguousarray(words), np.ascontiguousarray(byte.astype(np.uint8).reshape(n // 512, 16, m))


K, T, S, N, H = 512, 2048, 512, 512, 512


def setup_inputs():
    n = np.random.standard_normal
    s = mx_kscale(K)[:, None]
    u = mx_kscale(H)
    packed_xT = pack_weight(n((K, T)) * s)
    packed_w1 = pack_fp4(n((K, H)) / np.sqrt(K) / s)
    packed_w2 = pack_fp4(n((H, N)) / np.sqrt(H) / u[:, None])
    return {
        "x_words": packed_xT[0],
        "x_scales": packed_xT[1],
        "w1_words": packed_w1[0],
        "w1_scales": packed_w1[1],
        "gn": (np.random.uniform(0.5, 1.5, (H, 1)) * u[:, None]).astype(np.float32),
        "w2_words": packed_w2[0],
        "w2_scales": packed_w2[1],
        "offs": striped(np.random.permutation(T)[:S]),
        "t1": striped8(np.stack([np.random.permutation(S) for _ in range(8)])),
        "t2": striped8(np.stack([np.random.permutation(S) for _ in range(8)])),
        "t3": striped8(np.stack([np.random.permutation(S) for _ in range(8)])),
        "t4": striped8(np.stack([np.random.permutation(S) for _ in range(8)])),
    }


def reference(x_words, x_scales, w1_words, w1_scales, gn, w2_words, w2_scales, offs, t1, t2, t3, t4):
    xq = unpack_weight(x_words, x_scales)[:, unstriped(offs)]
    y = unpack_fp4(w1_words, w1_scales).T @ xq
    d1 = y[np.arange(H)[:, None], runs(t1, H)] - (y[np.arange(H)[:, None], runs(t2, H)])
    d2 = y[np.arange(H)[:, None], runs(t2, H)] - (y[np.arange(H)[:, None], runs(t3, H)])
    d3 = y[np.arange(H)[:, None], runs(t3, H)] - (y[np.arange(H)[:, None], runs(t4, H)])
    up = relu(d1) + relu(d2) + relu(d3)
    z = f64(gn) * (up / (np.abs(d1) + np.abs(d2) + np.abs(d3) + 0.25))
    out_0 = unpack_fp4(w2_words, w2_scales).T @ mxq(z, 0, "e4m3")
    return (out_0,) + planes(out_0)

@@ -1,0 +1,258 @@
+from contextlib import ExitStack
+
+import concourse.mybir as mybir
+from concourse.masks import make_identity
+
+K, T, S, H, N = 512, 2048, 512, 512, 512
+FLOPS = 2 * K * H * S + 2 * H * N * S
+
+F32 = mybir.dt.float32
+BF16 = mybir.dt.bfloat16
+I32 = mybir.dt.int32
+U32 = mybir.dt.uint32
+U16 = mybir.dt.uint16
+U8 = mybir.dt.uint8
+FP8X4 = mybir.dt.float8_e4m3fn_x4
+FP4X4 = mybir.dt.float4_e2m1fn_x4
+ALU = mybir.AluOpType
+ACT = mybir.ActivationFunctionType
+
+P = 128
+PACK = 4
+HALF = 256
+GW = 128
+
+
+def tile_picked_rsi4_none_po_kernel(
+    tc, x_words, x_scales, w1_words, w1_scales, gn, w2_words, w2_scales, offs, t1, t2, t3, t4, out_0, out_1, out_2
+):
+    nc = tc.nc
+    with ExitStack() as ctx:
+        keep = ctx.enter_context(tc.tile_pool(name="keep", bufs=1))
+        work = ctx.enter_context(tc.tile_pool(name="work", bufs=2))
+        psum = ctx.enter_context(tc.psum_pool(name="psum", bufs=1))
+
+        def load_scale_rows(tile, dram):
+            for q in range(4):
+                nc.sync.dma_start(out=tile[32 * q : 32 * q + 4, :].bitcast(I32), in_=dram[0, 4 * q : 4 * q + 4, :].bitcast(I32))
+
+        offs_sb = keep.tile([P, S // 16], U16, name="offs_sb")
+        x_table = keep.tile([P, T], I32, name="x_table", align_bytes=64)
+        xs_table = keep.tile([P, T], U8, name="xs_table", align_bytes=64)
+        w1_raw = keep.tile([P, 2 * H], U8, name="w1_raw", align_bytes=64)
+        w1s_raw = keep.tile([P, H], U8, name="w1s_raw", align_bytes=64)
+        w2_raw = keep.tile([P, 2 * N], U8, name="w2_raw", align_bytes=64)
+        w2s_raw = keep.tile([P, N], U8, name="w2s_raw", align_bytes=64)
+        gain = keep.tile([P, PACK], F32, name="gain")
+        quarter = keep.tile([P, 1], F32, name="quarter")
+
+        nc.vector.memset(w1s_raw[:].bitcast(I32), 0)
+        nc.vector.memset(w2s_raw[:].bitcast(I32), 0)
+
+        nc.scalar.dma_start(out=w1_raw[:].bitcast(I32), in_=w1_words[0].bitcast(I32))
+        nc.sync.dma_start(out=offs_sb[:], in_=offs)
+        for q in range(4):
+            rows = x_scales[0, 4 * q : 4 * q + 4, :].bitcast(I32)
+            nc.sync.dma_start(out=xs_table[32 * q : 32 * q + 32, :].bitcast(I32), in_=rows.unsqueeze(0).to_broadcast([8, 4, T // 4]))
+        nc.sync.dma_start(out=x_table[:], in_=x_words[0].rearrange("p n r -> p (n r)").bitcast(I32))
+        load_scale_rows(w1s_raw, w1_scales)
+        nc.sync.dma_start(out=gain[:], in_=gn.rearrange("(p t) o -> p (t o)", t=PACK))
+        lists = {}
+        for name, dram in (("n4", t4), ("p3", t3), ("n2", t2), ("p1", t1)):
+            tile = keep.tile([P, S // 16], U16, name=name + "_list")
+            nc.sync.dma_start(out=tile[:], in_=dram)
+            lists[name] = tile
+        nc.sync.dma_start(out=w2_raw[:].bitcast(I32), in_=w2_words[0].bitcast(I32))
+        load_scale_rows(w2s_raw, w2_scales)
+
+        nc.gpsimd.memset(quarter[:], 0.25)
+        ident = keep.tile([P, P], F32, name="ident")
+        make_identity(nc, ident[:])
+
+        w1_dealt = keep.tile([P, 2 * H], U8, name="w1_dealt", align_bytes=64)
+        w1s_dealt = keep.tile([P, H], U8, name="w1s_dealt", align_bytes=64)
+        w2_dealt = keep.tile([P, 2 * N], U8, name="w2_dealt", align_bytes=64)
+        w2s_dealt = keep.tile([P, N], U8, name="w2s_dealt", align_bytes=64)
+        nc.scalar.copy(
+            out=w1_dealt[:].bitcast(U16).rearrange("p (t m) -> p t m", t=PACK),
+            in_=w1_raw[:].bitcast(U16).rearrange("p (m t) -> p t m", t=PACK),
+        )
+        nc.vector.tensor_copy(
+            out=w1s_dealt[:].rearrange("p (t m) -> p t m", t=PACK),
+            in_=w1s_raw[:].rearrange("p (m t) -> p t m", t=PACK),
+        )
+        x_picked = []
+        xs_picked = []
+        for h in range(2):
+            half_list = offs_sb[:, 16 * h : 16 * h + 16]
+            tile = keep.tile([P, HALF], U8, name=f"xs_picked{h}", align_bytes=64)
+            nc.vector.tensor_copy(out=tile[:], in_=xs_table[:].indirect(half_list))
+            xs_picked.append(tile)
+            tile = keep.tile([P, HALF], U32, name=f"x_picked{h}", align_bytes=64)
+            nc.vector.tensor_copy(out=tile[:], in_=x_table[:].bitcast(U32).indirect(half_list))
+            x_picked.append(tile)
+        nc.gpsimd.tensor_copy(
+            out=w2_dealt[:].rearrange("p (t m b) -> p t m b", t=PACK, b=2),
+            in_=w2_raw[:].rearrange("p (m t b) -> p t m b", t=PACK, b=2),
+        )
+        nc.gpsimd.tensor_copy(
+            out=w2s_dealt[:].rearrange("p (t m) -> p t m", t=PACK),
+            in_=w2s_raw[:].rearrange("p (m t) -> p t m", t=PACK),
+        )
+
+        y = [keep.tile([P, S], F32, name=f"y{t}") for t in range(PACK)]
+        for h in range(2):
+            for tp in range(2):
+                bank = psum.tile([P, 2, HALF], F32, name=f"y_bank{h}{tp}", tag="fwd", bufs=5)
+                for tt in range(2):
+                    t = 2 * tp + tt
+                    nc.tensor.matmul_mx(
+                        out=bank[:, tt, :],
+                        lhsT=w1_dealt[:, 2 * P * t : 2 * P * (t + 1)].bitcast(FP4X4),
+                        lhsT_scale=w1s_dealt[:, P * t : P * (t + 1)],
+                        rhs=x_picked[h][:].bitcast(FP8X4),
+                        rhs_scale=xs_picked[h][:],
+                        start=True,
+                        stop=True,
+                    )
+                for tt in range(2):
+                    dst = y[2 * tp + tt][:, h * HALF : (h + 1) * HALF]
+                    if h == 1 and tp == 1:
+                        nc.vector.tensor_copy(out=dst, in_=bank[:, tt, :])
+                    else:
+                        nc.scalar.copy(out=dst, in_=bank[:, tt, :])
+
+        g = {}
+        on_scalar = lambda name, t, h: name in ("n4", "n2")
+
+        def gather(name, t, h):
+            tile = work.tile([P, GW], F32, name=f"{name}_{t}_{h}", tag=name, bufs=6)
+            window = y[t][:].indirect(lists[name][:, GW // 16 * h : GW // 16 * (h + 1)])
+            negate = name in ("n2", "n4")
+            if on_scalar(name, t, h):
+                nc.scalar.activation(out=tile[:], in_=window, func=ACT.Copy, scale=-1.0 if negate else 1.0)
+            elif negate:
+                nc.vector.tensor_scalar(out=tile[:], in0=window, scalar1=-1.0, scalar2=0.0, op0=ALU.mult, op1=ALU.add)
+            else:
+                nc.vector.tensor_copy(out=tile[:], in_=window)
+            g[name, t, h] = tile
+
+        span = {}
+
+        def gathers(h):
+            for t in range(PACK):
+                gather("n4", t, h)
+                gather("p3", t, h)
+            for t in range(PACK):
+                gather("n2", t, h)
+                gather("p1", t, h)
+            span[h] = work.tile([P, PACK, GW], F32, name=f"span{h}", tag="span", bufs=2)
+            for t in range(PACK):
+                nc.gpsimd.tensor_tensor(out=span[h][:, t, :], in0=g["p1", t, h][:], in1=g["n4", t, h][:], op=ALU.add)
+
+        def turned_sum(name, a, b, c):
+            h, jb = divmod(c * P, GW)
+            bank = psum.tile([P, PACK, P], F32, name=f"{name}{c}", tag="fwd", bufs=5)
+            for t in range(PACK):
+                for i, src in enumerate((a, b)):
+                    nc.tensor.matmul(
+                        out=bank[:, t, :],
+                        lhsT=g[src, t, h][:, jb : jb + P],
+                        rhs=ident[:],
+                        start=(i == 0),
+                        stop=(i == 1),
+                        is_transpose=True,
+                    )
+            return bank[:].rearrange("p b j -> p (b j)")
+
+        back = {}
+        zq = {}
+        out_codes = keep.tile([P, S], U32, name="out_codes", align_bytes=64)
+        out_scales = keep.tile([P, S], U8, name="out_scales", align_bytes=64)
+        out_rows = out_0.rearrange("(p t) j -> p t j", t=PACK)
+        out_words = out_1[0].rearrange("p n r -> p (n r)").bitcast(I32)
+
+        def rises(c):
+            d3 = turned_sum("d3_", "p3", "n4", c)
+            d1 = turned_sum("d1_", "p1", "n2", c)
+            nd2 = turned_sum("nd2_", "p3", "n2", c)
+            r3 = work.tile([P, S], F32, name="r3")
+            nc.scalar.activation(out=r3[:], in_=d3, func=ACT.Relu)
+            r13 = work.tile([P, S], F32, name="r13")
+            nc.vector.scalar_tensor_tensor(out=r13[:], in0=d1, scalar=0.0, in1=r3[:], op0=ALU.max, op1=ALU.add)
+            r2 = work.tile([P, S], F32, name="r2")
+            nc.scalar.activation(out=r2[:], in_=nd2, func=ACT.Relu, scale=-1.0)
+            back[c] = psum.tile([P, PACK, P], F32, name=f"back{c}", tag="back", bufs=2)
+            for t in range(PACK):
+                for i, src in enumerate((r13, r2)):
+                    nc.tensor.matmul(
+                        out=back[c][:, t, :], lhsT=src[:, t * P : (t + 1) * P], rhs=ident[:], start=(i == 0), stop=(i == 1), is_transpose=True
+                    )
+
+        def share(c):
+            h, jb = divmod(c * P, GW)
+            size = work.tile([P, PACK, P], F32, name="size")
+            nc.vector.scalar_tensor_tensor(
+                out=size[:], in0=back[c][:], scalar=2.0, in1=span[h][:, :, jb : jb + P], op0=ALU.mult, op1=ALU.subtract
+            )
+            root = work.tile([P, PACK, P], F32, name="root")
+            nc.scalar.activation(out=root[:], in_=size[:], func=ACT.Abs_reciprocal_sqrt, bias=quarter[:])
+            factor = work.tile([P, PACK, P], F32, name="factor")
+            for t in range(PACK):
+                nc.vector.scalar_tensor_tensor(
+                    out=factor[:, t, :], in0=root[:, t, :], scalar=gain[:, t : t + 1], in1=root[:, t, :], op0=ALU.mult, op1=ALU.mult
+                )
+            z = work.tile([P, P, PACK], BF16, name="z", align_bytes=64)
+            nc.vector.tensor_tensor(
+                out=z[:], in0=back[c][:].rearrange("p t j -> p j t"), in1=factor[:].rearrange("p t j -> p j t"), op=ALU.mult
+            )
+            z_codes = work.tile([P, P], U32, name="z_codes", align_bytes=64)
+            z_scales = work.tile([P, P], U8, name="z_scales", align_bytes=64)
+            nc.vector.quantize_mx(out=z_codes[:].bitcast(FP8X4), scales=z_scales[:], in_=z[:].rearrange("p j t -> p (j t)"))
+            zq[c] = (z_codes, z_scales)
+
+        def second_layer(c):
+            cols = slice(c * P, (c + 1) * P)
+            z_codes, z_scales = zq[c]
+            bank = psum.tile([P, PACK, P], F32, name=f"out_bank{c}", tag="out", bufs=1)
+            for t in range(PACK):
+                nc.tensor.matmul_mx(
+                    out=bank[:, t, :],
+                    lhsT=w2_dealt[:, 2 * P * t : 2 * P * (t + 1)].bitcast(FP4X4),
+                    lhsT_scale=w2s_dealt[:, P * t : P * (t + 1)],
+                    rhs=z_codes[:].bitcast(FP8X4),
+                    rhs_scale=z_scales[:],
+                    start=True,
+                    stop=True,
+                )
+            rounded = work.tile([P, P, PACK], BF16, name="rounded", align_bytes=64)
+            result = work.tile([P, PACK, P], F32, name="result")
+            nc.scalar.copy(out=rounded[:], in_=bank[:].rearrange("p t j -> p j t"))
+            nc.scalar.copy(out=result[:], in_=bank[:])
+            nc.vector.quantize_mx(
+                out=out_codes[:, cols].bitcast(FP8X4), scales=out_scales[:, cols], in_=rounded[:].rearrange("p j t -> p (j t)")
+            )
+            nc.sync.dma_start(out=out_rows[:, :, cols], in_=result[:])
+            nc.sync.dma_start(out=out_words[:, cols], in_=out_codes[:, cols].bitcast(I32))
+
+        gathers(0)
+        gathers(1)
+        rises(0)
+        gathers(2)
+        rises(1)
+        share(0)
+        gathers(3)
+        rises(2)
+        share(1)
+        second_layer(0)
+        rises(3)
+        share(2)
+        second_layer(1)
+        share(3)
+        second_layer(2)
+        second_layer(3)
+        for q in range(4):
+            queue = nc.sync if q % 2 == 0 else nc.scalar
+            queue.dma_start(
+                out=out_2[0, 4 * q : 4 * q + 4, :].bitcast(I32), in_=out_scales[32 * q : 32 * q + 4, :].bitcast(I32)
+            )

@@ -66,6 +66,8 @@ def tile_picked_rsi4_none_po_kernel(
         load_scale_rows(w2s_raw, w2_scales)
 
         nc.gpsimd.memset(quarter[:], 0.25)
+        warm = keep.tile([P, 1], F32, name="warm")
+        nc.scalar.activation(out=warm[:], in_=quarter[:], func=ACT.Abs_reciprocal_sqrt, bias=quarter[:])
         ident = keep.tile([P, P], F32, name="ident")
         make_identity(nc, ident[:])
 

@@ -19,8 +19,11 @@ ACT = mybir.ActivationFunctionType
 
 P = 128
 PACK = 4
-HALF = 256
-GW = 128
+HALF = S // 2
+CHUNKS = S // P
+QUADRANTS = 4
+LAST = PACK - 1
+UNITS = [(t, slice(0, S)) for t in range(LAST)] + [(LAST, slice(0, HALF)), (LAST, slice(HALF, S))]
 
 
 def tile_picked_rsi4_none_po_kernel(
@@ -29,11 +32,17 @@ def tile_picked_rsi4_none_po_kernel(
     nc = tc.nc
     with ExitStack() as ctx:
         keep = ctx.enter_context(tc.tile_pool(name="keep", bufs=1))
-        work = ctx.enter_context(tc.tile_pool(name="work", bufs=2))
+        work = ctx.enter_context(tc.tile_pool(name="work", bufs=CHUNKS))
         psum = ctx.enter_context(tc.psum_pool(name="psum", bufs=1))
 
+        def turned_bank(shape, name):
+            return psum.tile(shape, F32, name=name, tag="turned", bufs=4)
+
+        def back_bank(shape, name):
+            return psum.tile(shape, F32, name=name, tag="back", bufs=2)
+
         def load_scale_rows(tile, dram):
-            for q in range(4):
+            for q in range(QUADRANTS):
                 nc.sync.dma_start(out=tile[32 * q : 32 * q + 4, :].bitcast(I32), in_=dram[0, 4 * q : 4 * q + 4, :].bitcast(I32))
 
         offs_sb = keep.tile([P, S // 16], U16, name="offs_sb")
@@ -51,19 +60,19 @@ def tile_picked_rsi4_none_po_kernel(
 
         nc.scalar.dma_start(out=w1_raw[:].bitcast(I32), in_=w1_words[0].bitcast(I32))
         nc.sync.dma_start(out=offs_sb[:], in_=offs)
-        for q in range(4):
+        for q in range(QUADRANTS):
             rows = x_scales[0, 4 * q : 4 * q + 4, :].bitcast(I32)
             nc.sync.dma_start(out=xs_table[32 * q : 32 * q + 32, :].bitcast(I32), in_=rows.unsqueeze(0).to_broadcast([8, 4, T // 4]))
         nc.sync.dma_start(out=x_table[:], in_=x_words[0].rearrange("p n r -> p (n r)").bitcast(I32))
         load_scale_rows(w1s_raw, w1_scales)
-        nc.sync.dma_start(out=gain[:], in_=gn.rearrange("(p t) o -> p (t o)", t=PACK))
+        nc.sync.dma_start(out=w2_raw[:].bitcast(I32), in_=w2_words[0].bitcast(I32))
         lists = {}
         for name, dram in (("n4", t4), ("p3", t3), ("n2", t2), ("p1", t1)):
             tile = keep.tile([P, S // 16], U16, name=name + "_list")
             nc.sync.dma_start(out=tile[:], in_=dram)
             lists[name] = tile
-        nc.sync.dma_start(out=w2_raw[:].bitcast(I32), in_=w2_words[0].bitcast(I32))
         load_scale_rows(w2s_raw, w2_scales)
+        nc.sync.dma_start(out=gain[:], in_=gn.rearrange("(p t) o -> p (t o)", t=PACK))
 
         nc.gpsimd.memset(quarter[:], 0.25)
         warm = keep.tile([P, 1], F32, name="warm")
@@ -75,185 +84,173 @@ def tile_picked_rsi4_none_po_kernel(
         w1s_dealt = keep.tile([P, H], U8, name="w1s_dealt", align_bytes=64)
         w2_dealt = keep.tile([P, 2 * N], U8, name="w2_dealt", align_bytes=64)
         w2s_dealt = keep.tile([P, N], U8, name="w2s_dealt", align_bytes=64)
-        nc.scalar.copy(
-            out=w1_dealt[:].bitcast(U16).rearrange("p (t m) -> p t m", t=PACK),
-            in_=w1_raw[:].bitcast(U16).rearrange("p (m t) -> p t m", t=PACK),
-        )
-        nc.vector.tensor_copy(
-            out=w1s_dealt[:].rearrange("p (t m) -> p t m", t=PACK),
-            in_=w1s_raw[:].rearrange("p (m t) -> p t m", t=PACK),
-        )
+
+        def deal_words(dealt, raw):
+            nc.scalar.copy(
+                out=dealt[:].bitcast(U16).rearrange("p (t m) -> p t m", t=PACK),
+                in_=raw[:].bitcast(U16).rearrange("p (m t) -> p t m", t=PACK),
+            )
+
+        def deal_scales(dealt, raw):
+            nc.vector.tensor_copy(
+                out=dealt[:].rearrange("p (t m) -> p t m", t=PACK), in_=raw[:].rearrange("p (m t) -> p t m", t=PACK)
+            )
+
+        def mx_product(out, words, scales, t, codes, code_scales):
+            nc.tensor.matmul_mx(
+                out=out,
+                lhsT=words[:, 2 * P * t : 2 * P * (t + 1)].bitcast(FP4X4),
+                lhsT_scale=scales[:, P * t : P * (t + 1)],
+                rhs=codes[:].bitcast(FP8X4),
+                rhs_scale=code_scales[:],
+                start=True,
+                stop=True,
+            )
+
+        deal_words(w1_dealt, w1_raw)
+        deal_scales(w1s_dealt, w1s_raw)
+        deal_words(w2_dealt, w2_raw)
+
         x_picked = []
         xs_picked = []
         for h in range(2):
-            half_list = offs_sb[:, 16 * h : 16 * h + 16]
             tile = keep.tile([P, HALF], U8, name=f"xs_picked{h}", align_bytes=64)
-            nc.vector.tensor_copy(out=tile[:], in_=xs_table[:].indirect(half_list))
+            nc.vector.tensor_copy(out=tile[:], in_=xs_table[:].indirect(offs_sb[:, 16 * h : 16 * h + 16]))
             xs_picked.append(tile)
-            tile = keep.tile([P, HALF], U32, name=f"x_picked{h}", align_bytes=64)
-            nc.vector.tensor_copy(out=tile[:], in_=x_table[:].bitcast(U32).indirect(half_list))
-            x_picked.append(tile)
-        nc.gpsimd.tensor_copy(
-            out=w2_dealt[:].rearrange("p (t m b) -> p t m b", t=PACK, b=2),
-            in_=w2_raw[:].rearrange("p (m t b) -> p t m b", t=PACK, b=2),
-        )
-        nc.gpsimd.tensor_copy(
-            out=w2s_dealt[:].rearrange("p (t m) -> p t m", t=PACK),
-            in_=w2s_raw[:].rearrange("p (m t) -> p t m", t=PACK),
-        )
-
-        y = [keep.tile([P, S], F32, name=f"y{t}") for t in range(PACK)]
         for h in range(2):
-            for tp in range(2):
-                bank = psum.tile([P, 2, HALF], F32, name=f"y_bank{h}{tp}", tag="fwd", bufs=5)
-                for tt in range(2):
-                    t = 2 * tp + tt
-                    nc.tensor.matmul_mx(
-                        out=bank[:, tt, :],
-                        lhsT=w1_dealt[:, 2 * P * t : 2 * P * (t + 1)].bitcast(FP4X4),
-                        lhsT_scale=w1s_dealt[:, P * t : P * (t + 1)],
-                        rhs=x_picked[h][:].bitcast(FP8X4),
-                        rhs_scale=xs_picked[h][:],
-                        start=True,
-                        stop=True,
-                    )
-                for tt in range(2):
-                    dst = y[2 * tp + tt][:, h * HALF : (h + 1) * HALF]
-                    if h == 1 and tp == 1:
-                        nc.vector.tensor_copy(out=dst, in_=bank[:, tt, :])
+            tile = keep.tile([P, HALF], U32, name=f"x_picked{h}", align_bytes=64)
+            nc.vector.tensor_copy(out=tile[:], in_=x_table[:].bitcast(U32).indirect(offs_sb[:, 16 * h : 16 * h + 16]))
+            x_picked.append(tile)
+
+        y = [keep.tile([P, S if t == LAST else 2 * S], F32, name=f"y{t}") for t in range(PACK)]
+        for t in range(LAST):
+            nc.gpsimd.memset(y[t][:, S:], 0.0)
+        for pair in range(2):
+            bank = back_bank([P, 2, HALF], f"y_first{pair}")
+            for i in range(2):
+                mx_product(bank[:, i, :], w1_dealt, w1s_dealt, 2 * pair + i, x_picked[0], xs_picked[0])
+            for i in range(2):
+                nc.scalar.copy(out=y[2 * pair + i][:, :HALF], in_=bank[:, i, :])
+            for t in (2 * pair, 2 * pair + 1):
+                bank = turned_bank([P, HALF], f"y_second{t}")
+                mx_product(bank[:], w1_dealt, w1s_dealt, t, x_picked[1], xs_picked[1])
+                if t % 2 == 0:
+                    nc.scalar.copy(out=y[t][:, HALF:S], in_=bank[:])
+                else:
+                    nc.vector.tensor_copy(out=y[t][:, HALF:S], in_=bank[:])
+
+        def all_slices(name):
+            return keep.tile([P, PACK, S], F32, name=name)
+
+        picked = {name: all_slices("picked_" + name) for name in lists}
+        span, d1, up, size, root, factor = (all_slices(n) for n in ("span", "d1", "up", "size", "root", "factor"))
+
+        def gathers(t):
+            for cols in [cols for unit_t, cols in UNITS if unit_t == t]:
+                for name in ("n4", "p3", "n2", "p1"):
+                    window = y[t][:].indirect(lists[name][:, cols.start // 16 : cols.stop // 16])
+                    if name in ("n2", "n4"):
+                        nc.scalar.activation(out=picked[name][:, t, cols], in_=window, func=ACT.Copy, scale=-1.0)
                     else:
-                        nc.scalar.copy(out=dst, in_=bank[:, tt, :])
+                        nc.vector.tensor_copy(out=picked[name][:, t, cols], in_=window)
 
-        g = {}
-        on_scalar = lambda name, t, h: name in ("n4", "n2")
+        def add_turned(bank, a, b, width):
+            for j in range(0, width, P):
+                block = slice(j, j + P)
+                nc.tensor.matmul(out=bank[:, block], lhsT=a[:, block], rhs=ident[:], start=True, stop=False, is_transpose=True)
+                nc.tensor.matmul(out=bank[:, block], lhsT=b[:, block], rhs=ident[:], start=False, stop=True, is_transpose=True)
 
-        def gather(name, t, h):
-            tile = work.tile([P, GW], F32, name=f"{name}_{t}_{h}", tag=name, bufs=6)
-            window = y[t][:].indirect(lists[name][:, GW // 16 * h : GW // 16 * (h + 1)])
-            negate = name in ("n2", "n4")
-            if on_scalar(name, t, h):
-                nc.scalar.activation(out=tile[:], in_=window, func=ACT.Copy, scale=-1.0 if negate else 1.0)
-            elif negate:
-                nc.vector.tensor_scalar(out=tile[:], in0=window, scalar1=-1.0, scalar2=0.0, op0=ALU.mult, op1=ALU.add)
-            else:
-                nc.vector.tensor_copy(out=tile[:], in_=window)
-            g[name, t, h] = tile
+        def rises(u):
+            t, cols = UNITS[u]
+            width = cols.stop - cols.start
+            p1, n2, p3, n4 = (picked[name][:, t, cols] for name in ("p1", "n2", "p3", "n4"))
+            d3 = turned_bank([P, width], f"d3_{u}")
+            add_turned(d3, p3, n4, width)
+            minus_d2 = turned_bank([P, width], f"minus_d2_{u}")
+            add_turned(minus_d2, p3, n2, width)
+            r3 = work.tile([P, width], F32, name="r3")
+            nc.scalar.activation(out=r3[:], in_=d3[:], func=ACT.Relu, scale=1.0)
+            r2 = work.tile([P, width], F32, name="r2")
+            nc.scalar.activation(out=r2[:], in_=minus_d2[:], func=ACT.Relu, scale=-1.0)
+            r23 = back_bank([P, width], f"r23_{u}")
+            add_turned(r23, r3, r2, width)
+            adder = nc.vector if t == LAST else nc.gpsimd
+            adder.tensor_tensor(out=d1[:, t, cols], in0=p1, in1=n2, op=ALU.add)
+            adder.tensor_tensor(out=span[:, t, cols], in0=p1, in1=n4, op=ALU.add)
+            nc.vector.scalar_tensor_tensor(
+                out=up[:, t, cols], in0=d1[:, t, cols], scalar=0.0, in1=r23[:], op0=ALU.max, op1=ALU.add
+            )
 
-        span = {}
+        def divisor(u):
+            t, cols = UNITS[u]
+            nc.vector.scalar_tensor_tensor(
+                out=size[:, t, cols], in0=up[:, t, cols], scalar=2.0, in1=span[:, t, cols], op0=ALU.mult, op1=ALU.subtract
+            )
+            nc.scalar.activation(out=root[:, t, cols], in_=size[:, t, cols], func=ACT.Abs_reciprocal_sqrt, bias=quarter[:])
+            nc.vector.scalar_tensor_tensor(
+                out=factor[:, t, cols],
+                in0=root[:, t, cols],
+                scalar=gain[:, t : t + 1],
+                in1=root[:, t, cols],
+                op0=ALU.mult,
+                op1=ALU.mult,
+            )
 
-        def gathers(h):
-            for t in range(PACK):
-                gather("n4", t, h)
-                gather("p3", t, h)
-            for t in range(PACK):
-                gather("n2", t, h)
-                gather("p1", t, h)
-            span[h] = work.tile([P, PACK, GW], F32, name=f"span{h}", tag="span", bufs=2)
-            for t in range(PACK):
-                nc.gpsimd.tensor_tensor(out=span[h][:, t, :], in0=g["p1", t, h][:], in1=g["n4", t, h][:], op=ALU.add)
+        def by_slices(ap):
+            return ap.rearrange("p t (g i) -> p g t i", i=4)
 
-        def turned_sum(name, a, b, c):
-            h, jb = divmod(c * P, GW)
-            bank = psum.tile([P, PACK, P], F32, name=f"{name}{c}", tag="fwd", bufs=5)
-            for t in range(PACK):
-                for i, src in enumerate((a, b)):
-                    nc.tensor.matmul(
-                        out=bank[:, t, :],
-                        lhsT=g[src, t, h][:, jb : jb + P],
-                        rhs=ident[:],
-                        start=(i == 0),
-                        stop=(i == 1),
-                        is_transpose=True,
-                    )
-            return bank[:].rearrange("p b j -> p (b j)")
+        def by_places(ap):
+            return ap.rearrange("p (g i) t -> p g t i", i=4)
 
-        back = {}
-        zq = {}
+        z_mx = {}
+
+        def quantise_z(c):
+            cols = slice(c * P, (c + 1) * P)
+            z = work.tile([P, P, PACK], BF16, name="z", align_bytes=64)
+            nc.vector.tensor_tensor(
+                out=by_places(z[:]), in0=by_slices(up[:, :, cols]), in1=by_slices(factor[:, :, cols]), op=ALU.mult
+            )
+            z_codes = work.tile([P, P], U32, name="z_codes", align_bytes=64)
+            z_scales = work.tile([P, P], U8, name="z_scales", align_bytes=64)
+            nc.vector.quantize_mx(out=z_codes[:].bitcast(FP8X4), scales=z_scales[:], in_=z[:].rearrange("p j t -> p (j t)"))
+            z_mx[c] = (z_codes, z_scales)
+
         out_codes = keep.tile([P, S], U32, name="out_codes", align_bytes=64)
         out_scales = keep.tile([P, S], U8, name="out_scales", align_bytes=64)
         out_rows = out_0.rearrange("(p t) j -> p t j", t=PACK)
         out_words = out_1[0].rearrange("p n r -> p (n r)").bitcast(I32)
 
-        def rises(c):
-            d3 = turned_sum("d3_", "p3", "n4", c)
-            d1 = turned_sum("d1_", "p1", "n2", c)
-            nd2 = turned_sum("nd2_", "p3", "n2", c)
-            r3 = work.tile([P, S], F32, name="r3")
-            nc.scalar.activation(out=r3[:], in_=d3, func=ACT.Relu)
-            r13 = work.tile([P, S], F32, name="r13")
-            nc.vector.scalar_tensor_tensor(out=r13[:], in0=d1, scalar=0.0, in1=r3[:], op0=ALU.max, op1=ALU.add)
-            r2 = work.tile([P, S], F32, name="r2")
-            nc.scalar.activation(out=r2[:], in_=nd2, func=ACT.Relu, scale=-1.0)
-            back[c] = psum.tile([P, PACK, P], F32, name=f"back{c}", tag="back", bufs=2)
-            for t in range(PACK):
-                for i, src in enumerate((r13, r2)):
-                    nc.tensor.matmul(
-                        out=back[c][:, t, :], lhsT=src[:, t * P : (t + 1) * P], rhs=ident[:], start=(i == 0), stop=(i == 1), is_transpose=True
-                    )
-
-        def share(c):
-            h, jb = divmod(c * P, GW)
-            size = work.tile([P, PACK, P], F32, name="size")
-            nc.vector.scalar_tensor_tensor(
-                out=size[:], in0=back[c][:], scalar=2.0, in1=span[h][:, :, jb : jb + P], op0=ALU.mult, op1=ALU.subtract
-            )
-            root = work.tile([P, PACK, P], F32, name="root")
-            nc.scalar.activation(out=root[:], in_=size[:], func=ACT.Abs_reciprocal_sqrt, bias=quarter[:])
-            factor = work.tile([P, PACK, P], F32, name="factor")
-            for t in range(PACK):
-                nc.vector.scalar_tensor_tensor(
-                    out=factor[:, t, :], in0=root[:, t, :], scalar=gain[:, t : t + 1], in1=root[:, t, :], op0=ALU.mult, op1=ALU.mult
-                )
-            z = work.tile([P, P, PACK], BF16, name="z", align_bytes=64)
-            nc.vector.tensor_tensor(
-                out=z[:], in0=back[c][:].rearrange("p t j -> p j t"), in1=factor[:].rearrange("p t j -> p j t"), op=ALU.mult
-            )
-            z_codes = work.tile([P, P], U32, name="z_codes", align_bytes=64)
-            z_scales = work.tile([P, P], U8, name="z_scales", align_bytes=64)
-            nc.vector.quantize_mx(out=z_codes[:].bitcast(FP8X4), scales=z_scales[:], in_=z[:].rearrange("p j t -> p (j t)"))
-            zq[c] = (z_codes, z_scales)
-
-        def second_layer(c):
+        def second_product(c):
             cols = slice(c * P, (c + 1) * P)
-            z_codes, z_scales = zq[c]
-            bank = psum.tile([P, PACK, P], F32, name=f"out_bank{c}", tag="out", bufs=1)
+            bank = psum.tile([P, PACK, P], F32, name=f"out_bank{c}", tag="out", bufs=2)
             for t in range(PACK):
-                nc.tensor.matmul_mx(
-                    out=bank[:, t, :],
-                    lhsT=w2_dealt[:, 2 * P * t : 2 * P * (t + 1)].bitcast(FP4X4),
-                    lhsT_scale=w2s_dealt[:, P * t : P * (t + 1)],
-                    rhs=z_codes[:].bitcast(FP8X4),
-                    rhs_scale=z_scales[:],
-                    start=True,
-                    stop=True,
-                )
+                mx_product(bank[:, t, :], w2_dealt, w2s_dealt, t, *z_mx[c])
             rounded = work.tile([P, P, PACK], BF16, name="rounded", align_bytes=64)
             result = work.tile([P, PACK, P], F32, name="result")
-            nc.scalar.copy(out=rounded[:], in_=bank[:].rearrange("p t j -> p j t"))
-            nc.scalar.copy(out=result[:], in_=bank[:])
+            if c % 2 == 1:
+                nc.scalar.copy(out=result[:], in_=bank[:])
+                nc.vector.tensor_copy(out=by_places(rounded[:]), in_=by_slices(result[:]))
+            else:
+                nc.scalar.copy(out=rounded[:], in_=bank[:].rearrange("p t j -> p j t"))
+                nc.scalar.copy(out=result[:], in_=bank[:])
             nc.vector.quantize_mx(
                 out=out_codes[:, cols].bitcast(FP8X4), scales=out_scales[:, cols], in_=rounded[:].rearrange("p j t -> p (j t)")
             )
             nc.sync.dma_start(out=out_rows[:, :, cols], in_=result[:])
             nc.sync.dma_start(out=out_words[:, cols], in_=out_codes[:, cols].bitcast(I32))
 
-        gathers(0)
-        gathers(1)
-        rises(0)
-        gathers(2)
-        rises(1)
-        share(0)
-        gathers(3)
-        rises(2)
-        share(1)
-        second_layer(0)
-        rises(3)
-        share(2)
-        second_layer(1)
-        share(3)
-        second_layer(2)
-        second_layer(3)
-        for q in range(4):
+        deal_scales(w2s_dealt, w2s_raw)
+
+        for step in range(len(UNITS) + 3):
+            for stage, behind, count in ((gathers, 0, PACK), (divisor, 3, len(UNITS)), (rises, 1, len(UNITS))):
+                if 0 <= step - behind < count:
+                    stage(step - behind)
+        for step in range(CHUNKS + 1):
+            for stage, behind in ((quantise_z, 0), (second_product, 1)):
+                if 0 <= step - behind < CHUNKS:
+                    stage(step - behind)
+
+        for q in range(QUADRANTS):
             queue = nc.sync if q % 2 == 0 else nc.scalar
             queue.dma_start(
                 out=out_2[0, 4 * q : 4 * q + 4, :].bitcast(I32), in_=out_scales[32 * q : 32 * q + 4, :].bitcast(I32)

from contextlib import ExitStack

import concourse.mybir as mybir
from concourse.masks import make_identity

K, T, S, H, N = 512, 2048, 512, 512, 512
FLOPS = 2 * K * H * S + 2 * H * N * S

F32 = mybir.dt.float32
BF16 = mybir.dt.bfloat16
I32 = mybir.dt.int32
U32 = mybir.dt.uint32
U16 = mybir.dt.uint16
U8 = mybir.dt.uint8
FP8X4 = mybir.dt.float8_e4m3fn_x4
FP4X4 = mybir.dt.float4_e2m1fn_x4
ALU = mybir.AluOpType
ACT = mybir.ActivationFunctionType

P = 128
PACK = 4
HALF = S // 2
CHUNKS = S // P
QUADRANTS = 4
LAST = PACK - 1
UNITS = [(t, slice(0, S)) for t in range(LAST)] + [(LAST, slice(0, HALF)), (LAST, slice(HALF, S))]


def tile_picked_rsi4_none_po_kernel(
    tc, x_words, x_scales, w1_words, w1_scales, gn, w2_words, w2_scales, offs, t1, t2, t3, t4, out_0, out_1, out_2
):
    nc = tc.nc
    with ExitStack() as ctx:
        keep = ctx.enter_context(tc.tile_pool(name="keep", bufs=1))
        work = ctx.enter_context(tc.tile_pool(name="work", bufs=CHUNKS))
        psum = ctx.enter_context(tc.psum_pool(name="psum", bufs=1))

        def turned_bank(shape, name):
            return psum.tile(shape, F32, name=name, tag="turned", bufs=4)

        def back_bank(shape, name):
            return psum.tile(shape, F32, name=name, tag="back", bufs=2)

        def load_scale_rows(tile, dram):
            for q in range(QUADRANTS):
                nc.sync.dma_start(out=tile[32 * q : 32 * q + 4, :].bitcast(I32), in_=dram[0, 4 * q : 4 * q + 4, :].bitcast(I32))

        offs_sb = keep.tile([P, S // 16], U16, name="offs_sb")
        x_table = keep.tile([P, T], I32, name="x_table", align_bytes=64)
        xs_table = keep.tile([P, T], U8, name="xs_table", align_bytes=64)
        w1_raw = keep.tile([P, 2 * H], U8, name="w1_raw", align_bytes=64)
        w1s_raw = keep.tile([P, H], U8, name="w1s_raw", align_bytes=64)
        w2_raw = keep.tile([P, 2 * N], U8, name="w2_raw", align_bytes=64)
        w2s_raw = keep.tile([P, N], U8, name="w2s_raw", align_bytes=64)
        gain = keep.tile([P, PACK], F32, name="gain")
        quarter = keep.tile([P, 1], F32, name="quarter")

        nc.vector.memset(w1s_raw[:].bitcast(I32), 0)
        nc.vector.memset(w2s_raw[:].bitcast(I32), 0)

        nc.scalar.dma_start(out=w1_raw[:].bitcast(I32), in_=w1_words[0].bitcast(I32))
        nc.sync.dma_start(out=offs_sb[:], in_=offs)
        for q in range(QUADRANTS):
            rows = x_scales[0, 4 * q : 4 * q + 4, :].bitcast(I32)
            nc.sync.dma_start(out=xs_table[32 * q : 32 * q + 32, :].bitcast(I32), in_=rows.unsqueeze(0).to_broadcast([8, 4, T // 4]))
        nc.sync.dma_start(out=x_table[:], in_=x_words[0].rearrange("p n r -> p (n r)").bitcast(I32))
        load_scale_rows(w1s_raw, w1_scales)
        nc.sync.dma_start(out=w2_raw[:].bitcast(I32), in_=w2_words[0].bitcast(I32))
        lists = {}
        for name, dram in (("n4", t4), ("p3", t3), ("n2", t2), ("p1", t1)):
            tile = keep.tile([P, S // 16], U16, name=name + "_list")
            nc.sync.dma_start(out=tile[:], in_=dram)
            lists[name] = tile
        load_scale_rows(w2s_raw, w2_scales)
        nc.sync.dma_start(out=gain[:], in_=gn.rearrange("(p t) o -> p (t o)", t=PACK))

        nc.gpsimd.memset(quarter[:], 0.25)
        warm = keep.tile([P, 1], F32, name="warm")
        nc.scalar.activation(out=warm[:], in_=quarter[:], func=ACT.Abs_reciprocal_sqrt, bias=quarter[:])
        ident = keep.tile([P, P], F32, name="ident")
        make_identity(nc, ident[:])

        w1_dealt = keep.tile([P, 2 * H], U8, name="w1_dealt", align_bytes=64)
        w1s_dealt = keep.tile([P, H], U8, name="w1s_dealt", align_bytes=64)
        w2_dealt = keep.tile([P, 2 * N], U8, name="w2_dealt", align_bytes=64)
        w2s_dealt = keep.tile([P, N], U8, name="w2s_dealt", align_bytes=64)

        def deal_words(dealt, raw):
            nc.scalar.copy(
                out=dealt[:].bitcast(U16).rearrange("p (t m) -> p t m", t=PACK),
                in_=raw[:].bitcast(U16).rearrange("p (m t) -> p t m", t=PACK),
            )

        def deal_scales(dealt, raw):
            nc.vector.tensor_copy(
                out=dealt[:].rearrange("p (t m) -> p t m", t=PACK), in_=raw[:].rearrange("p (m t) -> p t m", t=PACK)
            )

        def mx_product(out, words, scales, t, codes, code_scales):
            nc.tensor.matmul_mx(
                out=out,
                lhsT=words[:, 2 * P * t : 2 * P * (t + 1)].bitcast(FP4X4),
                lhsT_scale=scales[:, P * t : P * (t + 1)],
                rhs=codes[:].bitcast(FP8X4),
                rhs_scale=code_scales[:],
                start=True,
                stop=True,
            )

        deal_words(w1_dealt, w1_raw)
        deal_scales(w1s_dealt, w1s_raw)
        deal_words(w2_dealt, w2_raw)

        x_picked = []
        xs_picked = []
        for h in range(2):
            tile = keep.tile([P, HALF], U8, name=f"xs_picked{h}", align_bytes=64)
            nc.vector.tensor_copy(out=tile[:], in_=xs_table[:].indirect(offs_sb[:, 16 * h : 16 * h + 16]))
            xs_picked.append(tile)
        for h in range(2):
            tile = keep.tile([P, HALF], U32, name=f"x_picked{h}", align_bytes=64)
            nc.vector.tensor_copy(out=tile[:], in_=x_table[:].bitcast(U32).indirect(offs_sb[:, 16 * h : 16 * h + 16]))
            x_picked.append(tile)

        y = [keep.tile([P, S if t == LAST else 2 * S], F32, name=f"y{t}") for t in range(PACK)]
        for t in range(LAST):
            nc.gpsimd.memset(y[t][:, S:], 0.0)
        for pair in range(2):
            bank = back_bank([P, 2, HALF], f"y_first{pair}")
            for i in range(2):
                mx_product(bank[:, i, :], w1_dealt, w1s_dealt, 2 * pair + i, x_picked[0], xs_picked[0])
            for i in range(2):
                nc.scalar.copy(out=y[2 * pair + i][:, :HALF], in_=bank[:, i, :])
            for t in (2 * pair, 2 * pair + 1):
                bank = turned_bank([P, HALF], f"y_second{t}")
                mx_product(bank[:], w1_dealt, w1s_dealt, t, x_picked[1], xs_picked[1])
                if t % 2 == 0:
                    nc.scalar.copy(out=y[t][:, HALF:S], in_=bank[:])
                else:
                    nc.vector.tensor_copy(out=y[t][:, HALF:S], in_=bank[:])

        def all_slices(name):
            return keep.tile([P, PACK, S], F32, name=name)

        picked = {name: all_slices("picked_" + name) for name in lists}
        span, d1, up, size, root, factor = (all_slices(n) for n in ("span", "d1", "up", "size", "root", "factor"))

        def gathers(t):
            for cols in [cols for unit_t, cols in UNITS if unit_t == t]:
                for name in ("n4", "p3", "n2", "p1"):
                    window = y[t][:].indirect(lists[name][:, cols.start // 16 : cols.stop // 16])
                    if name in ("n2", "n4"):
                        nc.scalar.activation(out=picked[name][:, t, cols], in_=window, func=ACT.Copy, scale=-1.0)
                    else:
                        nc.vector.tensor_copy(out=picked[name][:, t, cols], in_=window)

        def add_turned(bank, a, b, width):
            for j in range(0, width, P):
                block = slice(j, j + P)
                nc.tensor.matmul(out=bank[:, block], lhsT=a[:, block], rhs=ident[:], start=True, stop=False, is_transpose=True)
                nc.tensor.matmul(out=bank[:, block], lhsT=b[:, block], rhs=ident[:], start=False, stop=True, is_transpose=True)

        def rises(u):
            t, cols = UNITS[u]
            width = cols.stop - cols.start
            p1, n2, p3, n4 = (picked[name][:, t, cols] for name in ("p1", "n2", "p3", "n4"))
            d3 = turned_bank([P, width], f"d3_{u}")
            add_turned(d3, p3, n4, width)
            minus_d2 = turned_bank([P, width], f"minus_d2_{u}")
            add_turned(minus_d2, p3, n2, width)
            r3 = work.tile([P, width], F32, name="r3")
            nc.scalar.activation(out=r3[:], in_=d3[:], func=ACT.Relu, scale=1.0)
            r2 = work.tile([P, width], F32, name="r2")
            nc.scalar.activation(out=r2[:], in_=minus_d2[:], func=ACT.Relu, scale=-1.0)
            r23 = back_bank([P, width], f"r23_{u}")
            add_turned(r23, r3, r2, width)
            adder = nc.vector if t == LAST else nc.gpsimd
            adder.tensor_tensor(out=d1[:, t, cols], in0=p1, in1=n2, op=ALU.add)
            adder.tensor_tensor(out=span[:, t, cols], in0=p1, in1=n4, op=ALU.add)
            nc.vector.scalar_tensor_tensor(
                out=up[:, t, cols], in0=d1[:, t, cols], scalar=0.0, in1=r23[:], op0=ALU.max, op1=ALU.add
            )

        def divisor(u):
            t, cols = UNITS[u]
            nc.vector.scalar_tensor_tensor(
                out=size[:, t, cols], in0=up[:, t, cols], scalar=2.0, in1=span[:, t, cols], op0=ALU.mult, op1=ALU.subtract
            )
            nc.scalar.activation(out=root[:, t, cols], in_=size[:, t, cols], func=ACT.Abs_reciprocal_sqrt, bias=quarter[:])
            nc.vector.scalar_tensor_tensor(
                out=factor[:, t, cols],
                in0=root[:, t, cols],
                scalar=gain[:, t : t + 1],
                in1=root[:, t, cols],
                op0=ALU.mult,
                op1=ALU.mult,
            )

        def by_slices(ap):
            return ap.rearrange("p t (g i) -> p g t i", i=4)

        def by_places(ap):
            return ap.rearrange("p (g i) t -> p g t i", i=4)

        z_mx = {}

        def quantise_z(c):
            cols = slice(c * P, (c + 1) * P)
            z = work.tile([P, P, PACK], BF16, name="z", align_bytes=64)
            nc.vector.tensor_tensor(
                out=by_places(z[:]), in0=by_slices(up[:, :, cols]), in1=by_slices(factor[:, :, cols]), op=ALU.mult
            )
            z_codes = work.tile([P, P], U32, name="z_codes", align_bytes=64)
            z_scales = work.tile([P, P], U8, name="z_scales", align_bytes=64)
            nc.vector.quantize_mx(out=z_codes[:].bitcast(FP8X4), scales=z_scales[:], in_=z[:].rearrange("p j t -> p (j t)"))
            z_mx[c] = (z_codes, z_scales)

        out_codes = keep.tile([P, S], U32, name="out_codes", align_bytes=64)
        out_scales = keep.tile([P, S], U8, name="out_scales", align_bytes=64)
        out_rows = out_0.rearrange("(p t) j -> p t j", t=PACK)
        out_words = out_1[0].rearrange("p n r -> p (n r)").bitcast(I32)

        def second_product(c):
            cols = slice(c * P, (c + 1) * P)
            bank = psum.tile([P, PACK, P], F32, name=f"out_bank{c}", tag="out", bufs=2)
            for t in range(PACK):
                mx_product(bank[:, t, :], w2_dealt, w2s_dealt, t, *z_mx[c])
            rounded = work.tile([P, P, PACK], BF16, name="rounded", align_bytes=64)
            result = work.tile([P, PACK, P], F32, name="result")
            if c % 2 == 1:
                nc.scalar.copy(out=result[:], in_=bank[:])
                nc.vector.tensor_copy(out=by_places(rounded[:]), in_=by_slices(result[:]))
            else:
                nc.scalar.copy(out=rounded[:], in_=bank[:].rearrange("p t j -> p j t"))
                nc.scalar.copy(out=result[:], in_=bank[:])
            nc.vector.quantize_mx(
                out=out_codes[:, cols].bitcast(FP8X4), scales=out_scales[:, cols], in_=rounded[:].rearrange("p j t -> p (j t)")
            )
            nc.sync.dma_start(out=out_rows[:, :, cols], in_=result[:])
            nc.sync.dma_start(out=out_words[:, cols], in_=out_codes[:, cols].bitcast(I32))

        deal_scales(w2s_dealt, w2s_raw)

        for step in range(len(UNITS) + 3):
            for stage, behind, count in ((gathers, 0, PACK), (divisor, 3, len(UNITS)), (rises, 1, len(UNITS))):
                if 0 <= step - behind < count:
                    stage(step - behind)
        for step in range(CHUNKS + 1):
            for stage, behind in ((quantise_z, 0), (second_product, 1)):
                if 0 <= step - behind < CHUNKS:
                    stage(step - behind)

        for q in range(QUADRANTS):
            queue = nc.sync if q % 2 == 0 else nc.scalar
            queue.dma_start(
                out=out_2[0, 4 * q : 4 * q + 4, :].bitcast(I32), in_=out_scales[32 * q : 32 * q + 4, :].bitcast(I32)
            )
